import numpy as np
import ml_dtypes


def mxq(x, axis, fmt="e4m3"):
    dtype, down = {"e4m3": (ml_dtypes.float8_e4m3fn, 7), "e5m2": (ml_dtypes.float8_e5m2, 14)}[fmt]
    v = np.moveaxis(np.asarray(x, np.float32).astype(ml_dtypes.bfloat16).astype(np.float64), axis, -1)
    blocks = v.reshape(v.shape[:-1] + (-1, 32))
    amax = np.abs(blocks).max(-1, keepdims=True)
    byte = np.maximum(np.where(amax > 0, np.frexp(amax)[1] - 1 + 127, 0) - down, 1)
    scale = np.exp2(byte - 127.0)
    codes = (blocks / scale).astype(np.float32).astype(dtype).astype(np.float64)
    return np.moveaxis((codes * scale).reshape(v.shape), -1, axis)


WIDE = False


def mx_kscale(k):
    if not WIDE:
        return np.ones(k)
    levels = np.array([10, -10, 5, -5, 0])
    if k % 512:
        return np.exp2(np.random.permutation(np.resize(levels, k // 32))).repeat(32)
    a = np.empty((k // 512, 16))
    for p in range(k // 512):
        a[p, :8] = np.random.permutation(np.resize(levels, 8))
        for g in range(8):
            far = levels[np.abs(levels - a[p, g]) >= 10]
            a[p, g + 8] = far[np.random.randint(len(far))]
    return np.exp2(a.ravel()).repeat(32)


BF16 = ml_dtypes.bfloat16


def bf(x):
    return np.asarray(x, np.float32).astype(BF16)


def f64(x):
    return np.asarray(x).astype(np.float64)

def planes(Y):
    n, m = Y.shape
    b = f64(bf(Y)).reshape(n // 32, 32, m)
    amax = np.abs(b).max(1)
    byte = np.clip(np.where(amax > 0, np.frexp(amax)[1] - 1 + 127 - 7, 1), 1, 254)
    codes = (b * np.exp2(127.0 - byte)[:, None, :]).reshape(n, m).astype(np.float32).astype(ml_dtypes.float8_e4m3fn).view(np.uint8)
    words = codes.reshape(n // 512, 128, 4, m).transpose(0, 1, 3, 2)
    return np.ascontiguousarray(words), np.ascontiguousarray(byte.astype(np.uint8).reshape(n // 512, 16, m))


N, K, D, C = 1024, 1024, 1024, 512


def sigmoid(v):
    return 1.0 / (1.0 + np.exp(-v))


def loss_residual(z, y, c):
    return (sigmoid(z) - y) * c[None, :]


def setup_inputs():
    s, t = mx_kscale(D), mx_kscale(C)
    return {
        "xa": bf(np.random.standard_normal((N, D)) * s[None, :]),
        "w": bf(np.random.standard_normal((D, C)) / np.sqrt(D) / s[:, None]),
        "y": bf(np.random.uniform(0.0, 1.0, (N, C))),
        "c": bf((1.0 + 0.1 * np.random.standard_normal(C)) * t),
        "p": bf(1.0 + 0.1 * np.random.standard_normal(D)),
        "xb": bf(np.random.standard_normal((K, D)) / s[None, :]),
        "rb": bf(np.random.standard_normal((K, C)) / t[None, :]),
    }


def core(xa, w, y, c, p, xb, rb):
    xa64, p64 = f64(xa), f64(p)
    d = xa64.shape[1]
    n_classes = w.shape[1]
    z = mxq(xa64, 1, "e4m3") @ mxq(f64(w), 0, "e4m3")
    delta = loss_residual(z, f64(y), f64(c))
    s1 = mxq(xa64 * p64[None, :], 1, "e4m3") @ mxq(f64(xb), 1, "e4m3").T
    s2 = mxq(delta, 1, "e4m3") @ mxq(f64(rb), 1, "e4m3").T
    scale = 2.0 / np.sqrt(d * n_classes)
    return scale * s1 * s2


def reference(xa, w, y, c, p, xb, rb):
    R_out = core(xa, w, y, c, p, xb, rb)
    words, scales = planes(R_out)
    return R_out, words, scales

@@ -1,0 +1,426 @@
+from contextlib import ExitStack
+import math
+
+import concourse.mybir as mybir
+from concourse.masks import make_identity
+
+N, M, D, C = 1024, 1024, 1024, 512
+FLOPS = 2 * N * D * C + 2 * N * M * D + 2 * N * M * C
+
+F32 = mybir.dt.float32
+BF16 = mybir.dt.bfloat16
+I32 = mybir.dt.int32
+U32 = mybir.dt.uint32
+U8 = mybir.dt.uint8
+FP8X4 = mybir.dt.float8_e4m3fn_x4
+ACT = mybir.ActivationFunctionType
+ALU = mybir.AluOpType
+
+P = 128
+PACK = 4
+K_PASS = P * PACK
+BLK = 256
+BANK = 512
+N_BANKS = 8
+SCALE = 2.0 / math.sqrt(D * C)
+WARM_FIRST = 26
+WARM_SECOND = 12
+
+
+def tile_preconditionedtracininfluencematrix_x1_kernel(tc, xa, w, y, c, p, xb, rb, out_0, out_1, out_2):
+    nc = tc.nc
+    with ExitStack() as ctx:
+        sbuf = ctx.enter_context(tc.tile_pool(name="sbuf", bufs=1))
+        psum = ctx.enter_context(tc.psum_pool(name="psum", bufs=1))
+        ctx.enter_context(tc.manual_schedule())
+
+        made = {}
+
+        free_banks = list(range(N_BANKS))
+        bank_of = {}
+
+        def take_bank(key):
+            index = free_banks[0]
+            free_banks.remove(index)
+            bank = psum.tile([P, BANK], F32, name="bank%d" % index, tag="bank%d" % index)
+            bank_of[key] = index
+            made[key] = bank
+            return bank
+
+        def give_bank(key):
+            free_banks.append(bank_of[key])
+
+        def sb(tag, shape, dtype, bufs=1):
+            tile = sbuf.tile(shape, dtype, name=tag, tag=tag, bufs=bufs, align_bytes=64)
+            return tile
+
+        def quantize(key, values, words):
+            tag = "%s%d" % key
+            codes = sb(tag + "_codes", [P, words], U32)
+            scales = sb(tag + "_scales", [P, words], U8)
+            nc.vector.quantize_mx(out=codes[:].bitcast(FP8X4), scales=scales[:], in_=values[:])
+            made[key] = (codes, scales)
+
+        def matmul(out, stationary, s0, moving, m0, start, stop):
+            s_codes, s_scales = made[stationary]
+            m_codes, m_scales = made[moving]
+            nc.tensor.matmul_mx(
+                out=out,
+                lhsT=s_codes[:, s0:s0 + P].bitcast(FP8X4), lhsT_scale=s_scales[:, s0:s0 + P],
+                rhs=m_codes[:, m0:m0 + BLK].bitcast(FP8X4), rhs_scale=m_scales[:, m0:m0 + BLK],
+                start=start, stop=stop)
+
+        def transpose_words(key, raw, first_words):
+            bank = take_bank(key)
+            words = raw[:].bitcast(F32)
+            for s, first in enumerate(first_words):
+                nc.tensor.transpose(bank[:, P * s:P * (s + 1)], words[:, first:first + 2 * P - 1:2], ident[:])
+
+        def copy_words(grouped, key):
+            nc.scalar.copy(out=grouped.bitcast(F32).rearrange("q (i n u) -> q i n u", i=2, u=2),
+                           in_=made[key][:].rearrange("q (i u n) -> q i n u", i=2, u=2))
+            give_bank(key)
+
+
+        def load_w(h):
+            raw = sb("w%d" % h, [P, PACK * C], BF16)
+            rows = w[K_PASS * h:K_PASS * (h + 1), :]
+            nc.sync.dma_start(out=raw[:], in_=rows.rearrange("(q t) c -> q (t c)", t=PACK))
+            made["w", h] = raw
+
+        def load_xa(j):
+            g, half = divmod(j, 2)
+            raw = sb("xa%d" % j, [P, 2 * D], BF16)
+            rows = xa[K_PASS * g:K_PASS * (g + 1), :].rearrange("(q t) d -> q (t d)", t=PACK)
+            nc.sync.dma_start(out=raw[:], in_=rows[:, 2 * D * half:2 * D * (half + 1)])
+            made["xa", j] = raw
+
+        def load_y(g):
+            raw = sb("y%d" % g, [P, PACK * C], BF16)
+            rows = y[K_PASS * g:K_PASS * (g + 1), :]
+            nc.sync.dma_start(out=raw[:], in_=rows.rearrange("(q t) c -> q (t c)", t=PACK))
+            made["y", g] = raw
+
+        def load_xb(k):
+            raw = sb("xb%d" % k, [P, 2 * D], BF16)
+            rows = xb[BLK * k:BLK * (k + 1), :]
+            nc.sync.dma_start(out=raw[:].rearrange("q (i d) -> q i d", i=2), in_=rows.rearrange("(i q) d -> q i d", q=P))
+            made["xb", k] = raw
+
+        def load_rb(pair):
+            raw = sb("rb%d" % pair, [P, 4 * C], BF16)
+            rows = rb[2 * BLK * pair:2 * BLK * (pair + 1), :]
+            nc.sync.dma_start(out=raw[:].rearrange("q (i c) -> q i c", i=4), in_=rows.rearrange("(i q) c -> q i c", q=P))
+            made["rb", pair] = raw
+
+
+        def interleave_w(h):
+            grouped = sb("w_grouped%d" % h, [P, PACK * C], BF16)
+            nc.vector.tensor_copy(
+                out=grouped[:].rearrange("q (t a e r) -> q a t e r", t=PACK, e=2, r=PACK),
+                in_=made["w", h][:].rearrange("q (r a e t) -> q a t e r", r=PACK, e=2, t=PACK))
+            made["w_grouped", h] = grouped
+
+        def quantize_w(h):
+            quantize(("wq", h), made["w_grouped", h], C)
+
+        def turn_wide(kind, index, bufs):
+            for h in range(2):
+                firsts = [(D // 2) * i + (K_PASS // 2) * h + u for i in range(2) for u in range(2)]
+                transpose_words((kind + "_bank", index, h), made[kind, index], firsts)
+            grouped = sb(kind + "_grouped", [P, 2 * BLK * PACK], BF16, bufs)
+            for h in range(2):
+                copy_words(grouped[:, BLK * PACK * h:BLK * PACK * (h + 1)], (kind + "_bank", index, h))
+            made[kind + "_grouped", index] = grouped
+
+        def turn_xa(j):
+            turn_wide("xa", j, 4)
+
+        def turn_xb(k):
+            turn_wide("xb", k, 3)
+
+        def turn_rb(k):
+            firsts = [(C // 2) * (2 * (k % 2) + i) + u for i in range(2) for u in range(2)]
+            transpose_words(("rb_bank", k), made["rb", k // 2], firsts)
+            grouped = sb("rb_grouped", [P, BLK * PACK], BF16, 2)
+            copy_words(grouped[:], ("rb_bank", k))
+            made["rb_grouped", k] = grouped
+
+        def turn_y(j):
+            firsts = [(C // 2) * (2 * (j % 2) + i) + u for u in range(2) for i in range(2)]
+            transpose_words(("y_bank", j), made["y", j // 2], firsts)
+
+        def quantize_xa(j):
+            quantize(("xaq", j), made["xa_grouped", j], 2 * BLK)
+
+        def scale_xa(j):
+            scaled = sb("xp", [P, 2 * BLK * PACK], BF16, 2)
+            nc.vector.tensor_tensor(
+                out=scaled[:].rearrange("q (h n t) -> q h n t", h=2, t=PACK),
+                in0=made["xa_grouped", j][:].rearrange("q (h n t) -> q h n t", h=2, t=PACK),
+                in1=p_sb[:].unsqueeze(2).to_broadcast([P, 2, BLK, PACK]), op=ALU.mult)
+            made["xp", j] = scaled
+
+        def quantize_xp(j):
+            quantize(("xpq", j), made["xp", j], 2 * BLK)
+
+        def quantize_xb(k):
+            quantize(("xbq", k), made["xb_grouped", k], 2 * BLK)
+
+        def quantize_rb(k):
+            quantize(("rbq", k), made["rb_grouped", k], BLK)
+
+
+        def logits(j):
+            for u in range(2):
+                bank = take_bank(("z_bank", j, u))
+                for e in range(2):
+                    for h in range(2):
+                        matmul(bank[:, BLK * e:BLK * (e + 1)], ("wq", h), P * (2 * u + e), ("xaq", j), BLK * h,
+                               h == 0, h == 1)
+            sig = sb("sig", [P, 2 * BANK], F32, 2)
+            for u in range(2):
+                nc.scalar.activation(out=sig[:, BANK * u:BANK * (u + 1)].rearrange("q (n e) -> q n e", e=2),
+                                     in_=made["z_bank", j, u][:].rearrange("q (e n) -> q n e", e=2), func=ACT.Sigmoid)
+                give_bank(("z_bank", j, u))
+            made["sig", j] = sig
+
+        def subtract_y(j):
+            diff = sb("diff", [P, 2 * BANK], F32, 2)
+            nc.vector.tensor_tensor(out=diff[:], in0=made["sig", j][:], in1=made["y_bank", j][:].bitcast(BF16),
+                                    op=ALU.subtract)
+            give_bank(("y_bank", j))
+            made["diff", j] = diff
+
+        def scale_delta(j):
+            delta = sb("delta", [P, BLK * PACK], BF16, 2)
+            nc.vector.tensor_tensor(
+                out=delta[:].rearrange("q (n u e) -> q n u e", u=2, e=2),
+                in0=made["diff", j][:].rearrange("q (u n e) -> q n u e", u=2, e=2),
+                in1=c_sb[:].rearrange("q (u e) -> q u e", u=2).unsqueeze(1).to_broadcast([P, BLK, 2, 2]),
+                op=ALU.mult)
+            made["delta", j] = delta
+
+        def quantize_delta(j):
+            quantize(("dq", j), made["delta", j], BLK)
+
+
+        def similarity_1(j, k):
+            bank = take_bank(("s1_bank", j, k))
+            for i in range(2):
+                for h in range(2):
+                    matmul(bank[:, BLK * i:BLK * (i + 1)], ("xpq", j), BLK * h + P * i, ("xbq", k), BLK * h,
+                           h == 0, h == 1)
+            s1 = sb("s1", [P, BANK], F32, 8)
+            nc.scalar.activation(out=s1[:], in_=bank[:], func=ACT.Copy, scale=SCALE)
+            give_bank(("s1_bank", j, k))
+            made["s1", j, k] = s1
+
+        def similarity_2(j, k):
+            bank = take_bank(("s2_bank", j, k))
+            for i in range(2):
+                matmul(bank[:, BLK * i:BLK * (i + 1)], ("dq", j), P * i, ("rbq", k), 0, True, True)
+
+        def product(j, k):
+            g, half = divmod(j, 2)
+            if half == 0:
+                made["result", g, k] = sb("result", [P, PACK * BLK], F32, 4)
+            part = made["result", g, k][:, BANK * half:BANK * (half + 1)]
+            nc.vector.tensor_tensor(out=part, in0=made["s2_bank", j, k][:], in1=made["s1", j, k][:], op=ALU.mult)
+            give_bank(("s2_bank", j, k))
+            rows = out_0[K_PASS * g:K_PASS * (g + 1), BLK * k:BLK * (k + 1)].rearrange("(q t) m -> q t m", t=PACK)
+            nc.sync.dma_start(out=rows[:, 2 * half:2 * half + 2, :], in_=part.rearrange("q (t m) -> q t m", t=2))
+
+        def round_result(g, k, copy):
+            rounded = sb("rounded", [P, BLK * PACK], BF16, 4)
+            copy(out=rounded[:].rearrange("q (m r t) -> q m t r", r=4, t=PACK),
+                 in_=made["result", g, k][:].rearrange("q (t m r) -> q m t r", t=PACK, r=4))
+            made["rounded", g, k] = rounded
+
+        def quantize_result(g, k):
+            pair, half = divmod(k, 2)
+            if ("codes", g, pair) not in made:
+                made["codes", g, pair] = sb("out_codes%d_%d" % (g, pair), [P, 2 * BLK], U32)
+            codes = made["codes", g, pair][:, BLK * half:BLK * (half + 1)]
+            nc.vector.quantize_mx(out=codes.bitcast(FP8X4), scales=out_scales[4 * g:P, BLK * k:BLK * (k + 1)],
+                                  in_=made["rounded", g, k][:])
+
+        def store_codes(g, k0, k1):
+            codes = made["codes", g, k0 // 2][:, BLK * (k0 % 2):BLK * (k0 % 2 + k1 - k0)]
+            words = out_1[g].rearrange("q m t -> q (m t)").bitcast(I32)
+            nc.sync.dma_start(out=words[:, BLK * k0:BLK * k1], in_=codes.bitcast(I32))
+
+        def store_scales():
+            for quadrant in range(4):
+                queue = nc.scalar if quadrant % 2 == 0 else nc.sync
+                queue.dma_start(out=out_2[:, 4 * quadrant:4 * quadrant + 4, :].bitcast(I32),
+                                in_=out_scales[32 * quadrant:32 * quadrant + 8, :].bitcast(I32))
+
+        def warm_up(key, passes):
+            bank = take_bank(key)
+            codes, scales = made["zeroq", 0]
+            for s in range(passes):
+                nc.tensor.matmul_mx(out=bank[:, 0:P], lhsT=codes[:].bitcast(FP8X4), lhsT_scale=scales[:],
+                                    rhs=codes[:].bitcast(FP8X4), rhs_scale=scales[:], start=True, stop=True)
+            give_bank(key)
+
+
+        p_sb = sb("p_sb", [P, 2, PACK], BF16)
+        nc.scalar.dma_start(out=p_sb[:], in_=p.rearrange("(h q t) -> q h t", h=2, t=PACK))
+        c_sb = sb("c_sb", [P, PACK], BF16)
+        nc.scalar.dma_start(out=c_sb[:], in_=c.rearrange("(q t) -> q t", t=PACK))
+        zeros = sb("zeros", [P, K_PASS], BF16)
+        nc.vector.memset(zeros[:].bitcast(U32), 0)
+        quantize(("zeroq", 0), zeros, P)
+        ident = sb("ident", [P, P], F32)
+        make_identity(nc, ident[:])
+        table_load = sb("table_load", [P, 8], F32)
+        nc.scalar.activation(out=table_load[:], in_=zeros[:, 0:8], func=ACT.Sigmoid)
+        out_scales = sb("out_scales", [P, M], U8)
+
+        load_w(0)
+        load_xa(0)
+        load_w(1)
+        load_xa(1)
+        load_xb(0)
+        load_y(0)
+        load_rb(0)
+        load_xa(2)
+        load_xa(3)
+        load_xb(1)
+        load_xb(2)
+        load_rb(1)
+        load_y(1)
+        load_xb(3)
+
+
+        warm_up("warm_first", WARM_FIRST)
+        interleave_w(0)
+        quantize_w(0)
+        turn_xa(0)
+        interleave_w(1)
+        warm_up("warm_second", WARM_SECOND)
+        turn_xa(1)
+        turn_xb(0)
+        turn_y(0)
+        quantize_xa(0)
+        quantize_w(1)
+        scale_xa(0)
+        quantize_xa(1)
+
+        logits(0)
+        logits(1)
+        quantize_xp(0)
+        scale_xa(1)
+        quantize_xb(0)
+        quantize_xp(1)
+        turn_y(1)
+        turn_rb(0)
+        similarity_1(0, 0)
+        turn_xa(2)
+        turn_xa(3)
+        similarity_1(1, 0)
+        turn_xb(1)
+        turn_rb(1)
+        subtract_y(0)
+        subtract_y(1)
+        scale_delta(0)
+        quantize_rb(0)
+        scale_delta(1)
+        quantize_delta(0)
+        quantize_xa(2)
+        quantize_delta(1)
+
+        similarity_2(0, 0)
+        similarity_2(1, 0)
+        logits(2)
+        turn_xb(2)
+        turn_rb(2)
+        scale_xa(2)
+        quantize_xa(3)
+        product(0, 0)
+        quantize_xb(1)
+        similarity_1(0, 1)
+        turn_y(2)
+        turn_xb(3)
+        product(1, 0)
+        round_result(0, 0, nc.scalar.copy)
+        quantize_rb(1)
+        scale_xa(3)
+        similarity_1(1, 1)
+        turn_rb(3)
+        turn_y(3)
+        quantize_xp(2)
+        quantize_xb(2)
+        quantize_xp(3)
+        subtract_y(2)
+
+        logits(3)
+        for j in (0, 1):
+            similarity_2(j, 1)
+        for j in (0, 1):
+            similarity_1(j, 2)
+        quantize_rb(2)
+        quantize_xb(3)
+        scale_delta(2)
+        quantize_rb(3)
+        for j in (0, 1):
+            product(j, 1)
+        round_result(0, 1, nc.scalar.copy)
+        quantize_result(0, 0)
+        for j in (0, 1):
+            similarity_2(j, 2)
+        subtract_y(3)
+        quantize_delta(2)
+        for j in (0, 1):
+            similarity_1(j, 3)
+        for j in (2, 3):
+            similarity_1(j, 0)
+        for j in (0, 1):
+            similarity_2(j, 3)
+        scale_delta(3)
+        product(0, 2)
+        quantize_delta(3)
+        product(1, 2)
+
+        def matmuls_ahead(k):
+            for j in (2, 3):
+                similarity_1(j, k + 1)
+            for j in (2, 3):
+                similarity_2(j, k)
+
+        matmuls_ahead(0)
+        round_result(0, 2, nc.scalar.copy)
+        quantize_result(0, 1)
+        store_codes(0, 0, 2)
+        for j in (0, 1):
+            product(j, 3)
+        matmuls_ahead(1)
+        round_result(0, 3, nc.scalar.copy)
+        for j in (2, 3):
+            product(j, 0)
+        matmuls_ahead(2)
+        quantize_result(0, 2)
+        for j in (2, 3):
+            product(j, 1)
+        for j in (2, 3):
+            similarity_2(j, 3)
+        for k in (0, 1):
+            round_result(1, k, nc.scalar.copy)
+        for j in (2, 3):
+            product(j, 2)
+        quantize_result(0, 3)
+        store_codes(0, 2, 4)
+        for j in (2, 3):
+            product(j, 3)
+
+        round_result(1, 2, nc.vector.tensor_copy)
+        quantize_result(1, 0)
+        round_result(1, 3, nc.vector.tensor_copy)
+        quantize_result(1, 2)
+        store_codes(1, 2, 3)
+        quantize_result(1, 1)
+        store_codes(1, 0, 2)
+        quantize_result(1, 3)
+        store_codes(1, 3, 4)
+        store_scales()

@@ -23,8 +23,6 @@ BLK = 256
 BANK = 512
 N_BANKS = 8
 SCALE = 2.0 / math.sqrt(D * C)
-WARM_FIRST = 26
-WARM_SECOND = 12
 
 
 def tile_preconditionedtracininfluencematrix_x1_kernel(tc, xa, w, y, c, p, xb, rb, out_0, out_1, out_2):
@@ -223,26 +221,36 @@ def tile_preconditionedtracininfluencematrix_x1_kernel(tc, xa, w, y, c, p, xb, r
 
         def product(j, k):
             g, half = divmod(j, 2)
-            if half == 0:
-                made["result", g, k] = sb("result", [P, PACK * BLK], F32, 4)
-            part = made["result", g, k][:, BANK * half:BANK * (half + 1)]
-            nc.vector.tensor_tensor(out=part, in0=made["s2_bank", j, k][:], in1=made["s1", j, k][:], op=ALU.mult)
+            pair, side = divmod(k, 2)
+            if half == 0 and side == 0:
+                made["result", g, pair] = sb("result", [P, PACK, 2 * BLK], F32, 3)
+            part = made["result", g, pair][:, 2 * half:2 * half + 2, BLK * side:BLK * (side + 1)]
+            nc.vector.tensor_tensor(out=part, in0=made["s2_bank", j, k][:].rearrange("q (t m) -> q t m", t=2),
+                                    in1=made["s1", j, k][:].rearrange("q (t m) -> q t m", t=2), op=ALU.mult)
             give_bank(("s2_bank", j, k))
-            rows = out_0[K_PASS * g:K_PASS * (g + 1), BLK * k:BLK * (k + 1)].rearrange("(q t) m -> q t m", t=PACK)
-            nc.sync.dma_start(out=rows[:, 2 * half:2 * half + 2, :], in_=part.rearrange("q (t m) -> q t m", t=2))
+
+        def store_result(j, k0, k1):
+            g, half = divmod(j, 2)
+            part = made["result", g, k0 // 2][:, 2 * half:2 * half + 2, BLK * (k0 % 2):BLK * (k0 % 2 + k1 - k0)]
+            rows = out_0[K_PASS * g:K_PASS * (g + 1), BLK * k0:BLK * k1].rearrange("(q t) m -> q t m", t=PACK)
+            nc.sync.dma_start(out=rows[:, 2 * half:2 * half + 2, :], in_=part)
 
         def round_result(g, k, copy):
+            pair, side = divmod(k, 2)
             rounded = sb("rounded", [P, BLK * PACK], BF16, 4)
+            tile = made["result", g, pair][:, :, BLK * side:BLK * (side + 1)]
             copy(out=rounded[:].rearrange("q (m r t) -> q m t r", r=4, t=PACK),
-                 in_=made["result", g, k][:].rearrange("q (t m r) -> q m t r", t=PACK, r=4))
+                 in_=tile.rearrange("q t (m r) -> q m t r", r=4))
             made["rounded", g, k] = rounded
 
         def quantize_result(g, k):
             pair, half = divmod(k, 2)
             if ("codes", g, pair) not in made:
                 made["codes", g, pair] = sb("out_codes%d_%d" % (g, pair), [P, 2 * BLK], U32)
+            if "out_scales" not in made:
+                made["out_scales"] = sb("out_scales", [P, M], U8)
             codes = made["codes", g, pair][:, BLK * half:BLK * (half + 1)]
-            nc.vector.quantize_mx(out=codes.bitcast(FP8X4), scales=out_scales[4 * g:P, BLK * k:BLK * (k + 1)],
+            nc.vector.quantize_mx(out=codes.bitcast(FP8X4), scales=made["out_scales"][4 * g:P, BLK * k:BLK * (k + 1)],
                                   in_=made["rounded", g, k][:])
 
         def store_codes(g, k0, k1):
@@ -254,35 +262,25 @@ def tile_preconditionedtracininfluencematrix_x1_kernel(tc, xa, w, y, c, p, xb, r
             for quadrant in range(4):
                 queue = nc.scalar if quadrant % 2 == 0 else nc.sync
                 queue.dma_start(out=out_2[:, 4 * quadrant:4 * quadrant + 4, :].bitcast(I32),
-                                in_=out_scales[32 * quadrant:32 * quadrant + 8, :].bitcast(I32))
-
-        def warm_up(key, passes):
-            bank = take_bank(key)
-            codes, scales = made["zeroq", 0]
-            for s in range(passes):
-                nc.tensor.matmul_mx(out=bank[:, 0:P], lhsT=codes[:].bitcast(FP8X4), lhsT_scale=scales[:],
-                                    rhs=codes[:].bitcast(FP8X4), rhs_scale=scales[:], start=True, stop=True)
-            give_bank(key)
+                                in_=made["out_scales"][32 * quadrant:32 * quadrant + 8, :].bitcast(I32))
 
 
-        p_sb = sb("p_sb", [P, 2, PACK], BF16)
-        nc.scalar.dma_start(out=p_sb[:], in_=p.rearrange("(h q t) -> q h t", h=2, t=PACK))
-        c_sb = sb("c_sb", [P, PACK], BF16)
-        nc.scalar.dma_start(out=c_sb[:], in_=c.rearrange("(q t) -> q t", t=PACK))
-        zeros = sb("zeros", [P, K_PASS], BF16)
-        nc.vector.memset(zeros[:].bitcast(U32), 0)
-        quantize(("zeroq", 0), zeros, P)
         ident = sb("ident", [P, P], F32)
         make_identity(nc, ident[:])
+        zeros = sb("zeros", [P, 8], F32)
+        nc.vector.memset(zeros[:], 0.0)
         table_load = sb("table_load", [P, 8], F32)
-        nc.scalar.activation(out=table_load[:], in_=zeros[:, 0:8], func=ACT.Sigmoid)
-        out_scales = sb("out_scales", [P, M], U8)
+        nc.scalar.activation(out=table_load[:], in_=zeros[:], func=ACT.Sigmoid)
 
         load_w(0)
         load_xa(0)
         load_w(1)
+        p_sb = sb("p_sb", [P, 2, PACK], BF16)
+        nc.sync.dma_start(out=p_sb[:], in_=p.rearrange("(h q t) -> q h t", h=2, t=PACK))
         load_xa(1)
         load_xb(0)
+        c_sb = sb("c_sb", [P, PACK], BF16)
+        nc.sync.dma_start(out=c_sb[:], in_=c.rearrange("(q t) -> q t", t=PACK))
         load_y(0)
         load_rb(0)
         load_xa(2)
@@ -294,12 +292,10 @@ def tile_preconditionedtracininfluencematrix_x1_kernel(tc, xa, w, y, c, p, xb, r
         load_xb(3)
 
 
-        warm_up("warm_first", WARM_FIRST)
         interleave_w(0)
         quantize_w(0)
         turn_xa(0)
         interleave_w(1)
-        warm_up("warm_second", WARM_SECOND)
         turn_xa(1)
         turn_xb(0)
         turn_y(0)
@@ -310,18 +306,16 @@ def tile_preconditionedtracininfluencematrix_x1_kernel(tc, xa, w, y, c, p, xb, r
 
         logits(0)
         logits(1)
+        turn_y(1)
+        turn_rb(0)
+        turn_xa(2)
+        turn_xa(3)
+        turn_xb(1)
+        turn_rb(1)
         quantize_xp(0)
         scale_xa(1)
         quantize_xb(0)
         quantize_xp(1)
-        turn_y(1)
-        turn_rb(0)
-        similarity_1(0, 0)
-        turn_xa(2)
-        turn_xa(3)
-        similarity_1(1, 0)
-        turn_xb(1)
-        turn_rb(1)
         subtract_y(0)
         subtract_y(1)
         scale_delta(0)
@@ -331,23 +325,25 @@ def tile_preconditionedtracininfluencematrix_x1_kernel(tc, xa, w, y, c, p, xb, r
         quantize_xa(2)
         quantize_delta(1)
 
-        similarity_2(0, 0)
-        similarity_2(1, 0)
+        for j in (0, 1):
+            similarity_1(j, 0)
+        for j in (0, 1):
+            similarity_2(j, 0)
         logits(2)
         turn_xb(2)
         turn_rb(2)
+        turn_y(2)
+        turn_xb(3)
         scale_xa(2)
         quantize_xa(3)
         product(0, 0)
+        store_result(0, 0, 1)
         quantize_xb(1)
-        similarity_1(0, 1)
-        turn_y(2)
-        turn_xb(3)
         product(1, 0)
+        store_result(1, 0, 1)
         round_result(0, 0, nc.scalar.copy)
         quantize_rb(1)
         scale_xa(3)
-        similarity_1(1, 1)
         turn_rb(3)
         turn_y(3)
         quantize_xp(2)
@@ -355,64 +351,54 @@ def tile_preconditionedtracininfluencematrix_x1_kernel(tc, xa, w, y, c, p, xb, r
         quantize_xp(3)
         subtract_y(2)
 
+        def similarities(g, k):
+            for j in (2 * g, 2 * g + 1):
+                similarity_1(j, k)
+            for j in (2 * g, 2 * g + 1):
+                similarity_2(j, k)
+
+        def products(g, k, store_from):
+            for j in (2 * g, 2 * g + 1):
+                product(j, k)
+                if store_from <= k:
+                    store_result(j, store_from, k + 1)
+
         logits(3)
-        for j in (0, 1):
-            similarity_2(j, 1)
-        for j in (0, 1):
-            similarity_1(j, 2)
+        similarities(0, 1)
         quantize_rb(2)
         quantize_xb(3)
         scale_delta(2)
         quantize_rb(3)
-        for j in (0, 1):
-            product(j, 1)
-        round_result(0, 1, nc.scalar.copy)
         quantize_result(0, 0)
-        for j in (0, 1):
-            similarity_2(j, 2)
+        similarities(0, 2)
         subtract_y(3)
         quantize_delta(2)
-        for j in (0, 1):
-            similarity_1(j, 3)
-        for j in (2, 3):
-            similarity_1(j, 0)
-        for j in (0, 1):
-            similarity_2(j, 3)
+        products(0, 1, 1)
+        round_result(0, 1, nc.scalar.copy)
+        similarities(0, 3)
         scale_delta(3)
         product(0, 2)
         quantize_delta(3)
         product(1, 2)
 
-        def matmuls_ahead(k):
-            for j in (2, 3):
-                similarity_1(j, k + 1)
-            for j in (2, 3):
-                similarity_2(j, k)
-
-        matmuls_ahead(0)
+        similarities(1, 0)
         round_result(0, 2, nc.scalar.copy)
         quantize_result(0, 1)
         store_codes(0, 0, 2)
-        for j in (0, 1):
-            product(j, 3)
-        matmuls_ahead(1)
-        round_result(0, 3, nc.scalar.copy)
-        for j in (2, 3):
-            product(j, 0)
-        matmuls_ahead(2)
+        products(0, 3, 2)
+        similarities(1, 1)
+        products(1, 0, 1)
+        similarities(1, 2)
+        round_result(0, 3, nc.vector.tensor_copy)
         quantize_result(0, 2)
-        for j in (2, 3):
-            product(j, 1)
-        for j in (2, 3):
-            similarity_2(j, 3)
+        products(1, 1, 0)
+        similarities(1, 3)
         for k in (0, 1):
             round_result(1, k, nc.scalar.copy)
-        for j in (2, 3):
-            product(j, 2)
         quantize_result(0, 3)
         store_codes(0, 2, 4)
-        for j in (2, 3):
-            product(j, 3)
+        products(1, 2, 3)
+        products(1, 3, 2)
 
         round_result(1, 2, nc.vector.tensor_copy)
         quantize_result(1, 0)

from contextlib import ExitStack
import math

import concourse.mybir as mybir
from concourse.masks import make_identity

N, M, D, C = 1024, 1024, 1024, 512
FLOPS = 2 * N * D * C + 2 * N * M * D + 2 * N * M * C

F32 = mybir.dt.float32
BF16 = mybir.dt.bfloat16
I32 = mybir.dt.int32
U32 = mybir.dt.uint32
U8 = mybir.dt.uint8
FP8X4 = mybir.dt.float8_e4m3fn_x4
ACT = mybir.ActivationFunctionType
ALU = mybir.AluOpType

P = 128
PACK = 4
K_PASS = P * PACK
BLK = 256
BANK = 512
N_BANKS = 8
SCALE = 2.0 / math.sqrt(D * C)


def tile_preconditionedtracininfluencematrix_x1_kernel(tc, xa, w, y, c, p, xb, rb, out_0, out_1, out_2):
    nc = tc.nc
    with ExitStack() as ctx:
        sbuf = ctx.enter_context(tc.tile_pool(name="sbuf", bufs=1))
        psum = ctx.enter_context(tc.psum_pool(name="psum", bufs=1))
        ctx.enter_context(tc.manual_schedule())

        made = {}

        free_banks = list(range(N_BANKS))
        bank_of = {}

        def take_bank(key):
            index = free_banks[0]
            free_banks.remove(index)
            bank = psum.tile([P, BANK], F32, name="bank%d" % index, tag="bank%d" % index)
            bank_of[key] = index
            made[key] = bank
            return bank

        def give_bank(key):
            free_banks.append(bank_of[key])

        def sb(tag, shape, dtype, bufs=1):
            tile = sbuf.tile(shape, dtype, name=tag, tag=tag, bufs=bufs, align_bytes=64)
            return tile

        def quantize(key, values, words):
            tag = "%s%d" % key
            codes = sb(tag + "_codes", [P, words], U32)
            scales = sb(tag + "_scales", [P, words], U8)
            nc.vector.quantize_mx(out=codes[:].bitcast(FP8X4), scales=scales[:], in_=values[:])
            made[key] = (codes, scales)

        def matmul(out, stationary, s0, moving, m0, start, stop):
            s_codes, s_scales = made[stationary]
            m_codes, m_scales = made[moving]
            nc.tensor.matmul_mx(
                out=out,
                lhsT=s_codes[:, s0:s0 + P].bitcast(FP8X4), lhsT_scale=s_scales[:, s0:s0 + P],
                rhs=m_codes[:, m0:m0 + BLK].bitcast(FP8X4), rhs_scale=m_scales[:, m0:m0 + BLK],
                start=start, stop=stop)

        def transpose_words(key, raw, first_words):
            bank = take_bank(key)
            words = raw[:].bitcast(F32)
            for s, first in enumerate(first_words):
                nc.tensor.transpose(bank[:, P * s:P * (s + 1)], words[:, first:first + 2 * P - 1:2], ident[:])

        def copy_words(grouped, key):
            nc.scalar.copy(out=grouped.bitcast(F32).rearrange("q (i n u) -> q i n u", i=2, u=2),
                           in_=made[key][:].rearrange("q (i u n) -> q i n u", i=2, u=2))
            give_bank(key)


        def load_w(h):
            raw = sb("w%d" % h, [P, PACK * C], BF16)
            rows = w[K_PASS * h:K_PASS * (h + 1), :]
            nc.sync.dma_start(out=raw[:], in_=rows.rearrange("(q t) c -> q (t c)", t=PACK))
            made["w", h] = raw

        def load_xa(j):
            g, half = divmod(j, 2)
            raw = sb("xa%d" % j, [P, 2 * D], BF16)
            rows = xa[K_PASS * g:K_PASS * (g + 1), :].rearrange("(q t) d -> q (t d)", t=PACK)
            nc.sync.dma_start(out=raw[:], in_=rows[:, 2 * D * half:2 * D * (half + 1)])
            made["xa", j] = raw

        def load_y(g):
            raw = sb("y%d" % g, [P, PACK * C], BF16)
            rows = y[K_PASS * g:K_PASS * (g + 1), :]
            nc.sync.dma_start(out=raw[:], in_=rows.rearrange("(q t) c -> q (t c)", t=PACK))
            made["y", g] = raw

        def load_xb(k):
            raw = sb("xb%d" % k, [P, 2 * D], BF16)
            rows = xb[BLK * k:BLK * (k + 1), :]
            nc.sync.dma_start(out=raw[:].rearrange("q (i d) -> q i d", i=2), in_=rows.rearrange("(i q) d -> q i d", q=P))
            made["xb", k] = raw

        def load_rb(pair):
            raw = sb("rb%d" % pair, [P, 4 * C], BF16)
            rows = rb[2 * BLK * pair:2 * BLK * (pair + 1), :]
            nc.sync.dma_start(out=raw[:].rearrange("q (i c) -> q i c", i=4), in_=rows.rearrange("(i q) c -> q i c", q=P))
            made["rb", pair] = raw


        def interleave_w(h):
            grouped = sb("w_grouped%d" % h, [P, PACK * C], BF16)
            nc.vector.tensor_copy(
                out=grouped[:].rearrange("q (t a e r) -> q a t e r", t=PACK, e=2, r=PACK),
                in_=made["w", h][:].rearrange("q (r a e t) -> q a t e r", r=PACK, e=2, t=PACK))
            made["w_grouped", h] = grouped

        def quantize_w(h):
            quantize(("wq", h), made["w_grouped", h], C)

        def turn_wide(kind, index, bufs):
            for h in range(2):
                firsts = [(D // 2) * i + (K_PASS // 2) * h + u for i in range(2) for u in range(2)]
                transpose_words((kind + "_bank", index, h), made[kind, index], firsts)
            grouped = sb(kind + "_grouped", [P, 2 * BLK * PACK], BF16, bufs)
            for h in range(2):
                copy_words(grouped[:, BLK * PACK * h:BLK * PACK * (h + 1)], (kind + "_bank", index, h))
            made[kind + "_grouped", index] = grouped

        def turn_xa(j):
            turn_wide("xa", j, 4)

        def turn_xb(k):
            turn_wide("xb", k, 3)

        def turn_rb(k):
            firsts = [(C // 2) * (2 * (k % 2) + i) + u for i in range(2) for u in range(2)]
            transpose_words(("rb_bank", k), made["rb", k // 2], firsts)
            grouped = sb("rb_grouped", [P, BLK * PACK], BF16, 2)
            copy_words(grouped[:], ("rb_bank", k))
            made["rb_grouped", k] = grouped

        def turn_y(j):
            firsts = [(C // 2) * (2 * (j % 2) + i) + u for u in range(2) for i in range(2)]
            transpose_words(("y_bank", j), made["y", j // 2], firsts)

        def quantize_xa(j):
            quantize(("xaq", j), made["xa_grouped", j], 2 * BLK)

        def scale_xa(j):
            scaled = sb("xp", [P, 2 * BLK * PACK], BF16, 2)
            nc.vector.tensor_tensor(
                out=scaled[:].rearrange("q (h n t) -> q h n t", h=2, t=PACK),
                in0=made["xa_grouped", j][:].rearrange("q (h n t) -> q h n t", h=2, t=PACK),
                in1=p_sb[:].unsqueeze(2).to_broadcast([P, 2, BLK, PACK]), op=ALU.mult)
            made["xp", j] = scaled

        def quantize_xp(j):
            quantize(("xpq", j), made["xp", j], 2 * BLK)

        def quantize_xb(k):
            quantize(("xbq", k), made["xb_grouped", k], 2 * BLK)

        def quantize_rb(k):
            quantize(("rbq", k), made["rb_grouped", k], BLK)


        def logits(j):
            for u in range(2):
                bank = take_bank(("z_bank", j, u))
                for e in range(2):
                    for h in range(2):
                        matmul(bank[:, BLK * e:BLK * (e + 1)], ("wq", h), P * (2 * u + e), ("xaq", j), BLK * h,
                               h == 0, h == 1)
            sig = sb("sig", [P, 2 * BANK], F32, 2)
            for u in range(2):
                nc.scalar.activation(out=sig[:, BANK * u:BANK * (u + 1)].rearrange("q (n e) -> q n e", e=2),
                                     in_=made["z_bank", j, u][:].rearrange("q (e n) -> q n e", e=2), func=ACT.Sigmoid)
                give_bank(("z_bank", j, u))
            made["sig", j] = sig

        def subtract_y(j):
            diff = sb("diff", [P, 2 * BANK], F32, 2)
            nc.vector.tensor_tensor(out=diff[:], in0=made["sig", j][:], in1=made["y_bank", j][:].bitcast(BF16),
                                    op=ALU.subtract)
            give_bank(("y_bank", j))
            made["diff", j] = diff

        def scale_delta(j):
            delta = sb("delta", [P, BLK * PACK], BF16, 2)
            nc.vector.tensor_tensor(
                out=delta[:].rearrange("q (n u e) -> q n u e", u=2, e=2),
                in0=made["diff", j][:].rearrange("q (u n e) -> q n u e", u=2, e=2),
                in1=c_sb[:].rearrange("q (u e) -> q u e", u=2).unsqueeze(1).to_broadcast([P, BLK, 2, 2]),
                op=ALU.mult)
            made["delta", j] = delta

        def quantize_delta(j):
            quantize(("dq", j), made["delta", j], BLK)


        def similarity_1(j, k):
            bank = take_bank(("s1_bank", j, k))
            for i in range(2):
                for h in range(2):
                    matmul(bank[:, BLK * i:BLK * (i + 1)], ("xpq", j), BLK * h + P * i, ("xbq", k), BLK * h,
                           h == 0, h == 1)
            s1 = sb("s1", [P, BANK], F32, 8)
            nc.scalar.activation(out=s1[:], in_=bank[:], func=ACT.Copy, scale=SCALE)
            give_bank(("s1_bank", j, k))
            made["s1", j, k] = s1

        def similarity_2(j, k):
            bank = take_bank(("s2_bank", j, k))
            for i in range(2):
                matmul(bank[:, BLK * i:BLK * (i + 1)], ("dq", j), P * i, ("rbq", k), 0, True, True)

        def product(j, k):
            g, half = divmod(j, 2)
            pair, side = divmod(k, 2)
            if half == 0 and side == 0:
                made["result", g, pair] = sb("result", [P, PACK, 2 * BLK], F32, 3)
            part = made["result", g, pair][:, 2 * half:2 * half + 2, BLK * side:BLK * (side + 1)]
            nc.vector.tensor_tensor(out=part, in0=made["s2_bank", j, k][:].rearrange("q (t m) -> q t m", t=2),
                                    in1=made["s1", j, k][:].rearrange("q (t m) -> q t m", t=2), op=ALU.mult)
            give_bank(("s2_bank", j, k))

        def store_result(j, k0, k1):
            g, half = divmod(j, 2)
            part = made["result", g, k0 // 2][:, 2 * half:2 * half + 2, BLK * (k0 % 2):BLK * (k0 % 2 + k1 - k0)]
            rows = out_0[K_PASS * g:K_PASS * (g + 1), BLK * k0:BLK * k1].rearrange("(q t) m -> q t m", t=PACK)
            nc.sync.dma_start(out=rows[:, 2 * half:2 * half + 2, :], in_=part)

        def round_result(g, k, copy):
            pair, side = divmod(k, 2)
            rounded = sb("rounded", [P, BLK * PACK], BF16, 4)
            tile = made["result", g, pair][:, :, BLK * side:BLK * (side + 1)]
            copy(out=rounded[:].rearrange("q (m r t) -> q m t r", r=4, t=PACK),
                 in_=tile.rearrange("q t (m r) -> q m t r", r=4))
            made["rounded", g, k] = rounded

        def quantize_result(g, k):
            pair, half = divmod(k, 2)
            if ("codes", g, pair) not in made:
                made["codes", g, pair] = sb("out_codes%d_%d" % (g, pair), [P, 2 * BLK], U32)
            if "out_scales" not in made:
                made["out_scales"] = sb("out_scales", [P, M], U8)
            codes = made["codes", g, pair][:, BLK * half:BLK * (half + 1)]
            nc.vector.quantize_mx(out=codes.bitcast(FP8X4), scales=made["out_scales"][4 * g:P, BLK * k:BLK * (k + 1)],
                                  in_=made["rounded", g, k][:])

        def store_codes(g, k0, k1):
            codes = made["codes", g, k0 // 2][:, BLK * (k0 % 2):BLK * (k0 % 2 + k1 - k0)]
            words = out_1[g].rearrange("q m t -> q (m t)").bitcast(I32)
            nc.sync.dma_start(out=words[:, BLK * k0:BLK * k1], in_=codes.bitcast(I32))

        def store_scales():
            for quadrant in range(4):
                queue = nc.scalar if quadrant % 2 == 0 else nc.sync
                queue.dma_start(out=out_2[:, 4 * quadrant:4 * quadrant + 4, :].bitcast(I32),
                                in_=made["out_scales"][32 * quadrant:32 * quadrant + 8, :].bitcast(I32))


        ident = sb("ident", [P, P], F32)
        make_identity(nc, ident[:])
        zeros = sb("zeros", [P, 8], F32)
        nc.vector.memset(zeros[:], 0.0)
        table_load = sb("table_load", [P, 8], F32)
        nc.scalar.activation(out=table_load[:], in_=zeros[:], func=ACT.Sigmoid)

        load_w(0)
        load_xa(0)
        load_w(1)
        p_sb = sb("p_sb", [P, 2, PACK], BF16)
        nc.sync.dma_start(out=p_sb[:], in_=p.rearrange("(h q t) -> q h t", h=2, t=PACK))
        load_xa(1)
        load_xb(0)
        c_sb = sb("c_sb", [P, PACK], BF16)
        nc.sync.dma_start(out=c_sb[:], in_=c.rearrange("(q t) -> q t", t=PACK))
        load_y(0)
        load_rb(0)
        load_xa(2)
        load_xa(3)
        load_xb(1)
        load_xb(2)
        load_rb(1)
        load_y(1)
        load_xb(3)


        interleave_w(0)
        quantize_w(0)
        turn_xa(0)
        interleave_w(1)
        turn_xa(1)
        turn_xb(0)
        turn_y(0)
        quantize_xa(0)
        quantize_w(1)
        scale_xa(0)
        quantize_xa(1)

        logits(0)
        logits(1)
        turn_y(1)
        turn_rb(0)
        turn_xa(2)
        turn_xa(3)
        turn_xb(1)
        turn_rb(1)
        quantize_xp(0)
        scale_xa(1)
        quantize_xb(0)
        quantize_xp(1)
        subtract_y(0)
        subtract_y(1)
        scale_delta(0)
        quantize_rb(0)
        scale_delta(1)
        quantize_delta(0)
        quantize_xa(2)
        quantize_delta(1)

        for j in (0, 1):
            similarity_1(j, 0)
        for j in (0, 1):
            similarity_2(j, 0)
        logits(2)
        turn_xb(2)
        turn_rb(2)
        turn_y(2)
        turn_xb(3)
        scale_xa(2)
        quantize_xa(3)
        product(0, 0)
        store_result(0, 0, 1)
        quantize_xb(1)
        product(1, 0)
        store_result(1, 0, 1)
        round_result(0, 0, nc.scalar.copy)
        quantize_rb(1)
        scale_xa(3)
        turn_rb(3)
        turn_y(3)
        quantize_xp(2)
        quantize_xb(2)
        quantize_xp(3)
        subtract_y(2)

        def similarities(g, k):
            for j in (2 * g, 2 * g + 1):
                similarity_1(j, k)
            for j in (2 * g, 2 * g + 1):
                similarity_2(j, k)

        def products(g, k, store_from):
            for j in (2 * g, 2 * g + 1):
                product(j, k)
                if store_from <= k:
                    store_result(j, store_from, k + 1)

        logits(3)
        similarities(0, 1)
        quantize_rb(2)
        quantize_xb(3)
        scale_delta(2)
        quantize_rb(3)
        quantize_result(0, 0)
        similarities(0, 2)
        subtract_y(3)
        quantize_delta(2)
        products(0, 1, 1)
        round_result(0, 1, nc.scalar.copy)
        similarities(0, 3)
        scale_delta(3)
        product(0, 2)
        quantize_delta(3)
        product(1, 2)

        similarities(1, 0)
        round_result(0, 2, nc.scalar.copy)
        quantize_result(0, 1)
        store_codes(0, 0, 2)
        products(0, 3, 2)
        similarities(1, 1)
        products(1, 0, 1)
        similarities(1, 2)
        round_result(0, 3, nc.vector.tensor_copy)
        quantize_result(0, 2)
        products(1, 1, 0)
        similarities(1, 3)
        for k in (0, 1):
            round_result(1, k, nc.scalar.copy)
        quantize_result(0, 3)
        store_codes(0, 2, 4)
        products(1, 2, 3)
        products(1, 3, 2)

        round_result(1, 2, nc.vector.tensor_copy)
        quantize_result(1, 0)
        round_result(1, 3, nc.vector.tensor_copy)
        quantize_result(1, 2)
        store_codes(1, 2, 3)
        quantize_result(1, 1)
        store_codes(1, 0, 2)
        quantize_result(1, 3)
        store_codes(1, 3, 4)
        store_scales()
